import numpy as np, ml_dtypes
CORES = [2,34,66,98,130,162,194,226,258,290,322,354,386,418,450,482]
N = 16
CB = 1
def setup_inputs(rng):
    k = (rng.standard_normal((N, 128, CB * 128), dtype=np.float32) / 8).astype(ml_dtypes.bfloat16)
    kt = np.concatenate([k[:, :, 128 * c:128 * c + 128].transpose(0, 2, 1) for c in range(CB)], axis=2)
    tri = np.triu(np.ones((128, 128), np.float32)).astype(ml_dtypes.bfloat16)
    return {"q": (rng.standard_normal((N, 128, CB * 128), dtype=np.float32) / 8).astype(ml_dtypes.bfloat16), "k": k, "kt": kt, "v": rng.standard_normal((N, 128, CB * 128), dtype=np.float32).astype(ml_dtypes.bfloat16), "m": np.broadcast_to(tri, (N, 128, 128)).copy()}
def setup_inputs_big(rng):
    d = setup_inputs(rng)
    for k in ("q", "k", "kt", "v"): d[k] = (d[k].astype(np.float32) * 1024.0).astype(d[k].dtype)
    return d
def setup_inputs_small(rng):
    d = setup_inputs(rng)
    for k in ("q", "k", "kt", "v"): d[k] = (d[k].astype(np.float32) * (1 / 1024.0)).astype(d[k].dtype)
    return d
def setup_inputs_apart(rng):
    d = setup_inputs(rng)
    f = (10.0 ** rng.permutation(np.linspace(-1.5, 1.5, N))).astype(np.float32).reshape(N, 1, 1)
    for k in ("q", "k", "kt", "v"): d[k] = (d[k].astype(np.float32) * f).astype(d[k].dtype)
    return d
def reference(q, k, kt, v, m):
    Q, K, KT, V, M = q.astype(np.float64), k.astype(np.float64), kt.astype(np.float64), v.astype(np.float64), m.astype(np.float64)
    y = np.zeros((N, 128, CB * 128)); Z = np.zeros((128, 128))
    for r in range(N):
        for c in range(CB):
            s = slice(128 * c, 128 * c + 128)
            y[r][:, s] = Z.T @ Q[r][:, s] + V[r][:, s].T @ ((K[r][:, s].T @ Q[r][:, s]) * M[r])
            Z = Z + KT[r][:, s].T @ V[r][:, s]
    return {"y": y.astype(ml_dtypes.bfloat16)}

@@ -1,0 +1,169 @@
+from concourse.bass import DstId, RemoteDMATransfer
+from concourse.mybir import AluOpType
+
+B = 128
+NSLOT = 11
+SCRATCH = {
+    "kt_sb": ("sbuf", [B, B], "bfloat16"),
+    "v_sb": ("sbuf", [B, B], "bfloat16"),
+    "q_sb": ("sbuf", [B, B], "bfloat16"),
+    "k_sb": ("sbuf", [B, B], "bfloat16"),
+    "m_sb": ("sbuf", [B, B], "bfloat16"),
+    "s_bf": ("sbuf", [B, B], "bfloat16"),
+    "am_bf": ("sbuf", [B, B], "bfloat16"),
+    "gs_bf": ("sbuf", [B, B], "bfloat16"),
+    "y_sb": ("sbuf", [B, B], "bfloat16"),
+    "land": ("sbuf", [B, NSLOT * B], "bfloat16"),
+    "ps_s": ("psum", [B, 512], "float32"),
+    "ps_a": ("psum", [B, 512], "float32"),
+    "ps_y": ("psum", [B, 512], "float32"),
+    "ps_c": ("psum", [B, 512], "float32"),
+}
+SEMAPHORES = ["lkv", "lqk", "lm", "ps", "pa", "py", "vs", "va", "vc", "vg", "vy", "sty", "sent",
+              "sg0", "sg1", "sg2", "sg3", "sw", "st0", "st1", "sh"]
+
+
+def _plan(cores, topo):
+    n = len(cores)
+    hosts = []
+    for r, c in enumerate(cores):
+        if not hosts or topo.host(cores[hosts[-1][0]]) != topo.host(c):
+            hosts.append([])
+        hosts[-1].append(r)
+    pos = {r: i for rs in hosts for i, r in enumerate(rs)}
+    rack_of = lambda rs: topo.rack(topo.host(cores[rs[0]]))
+    near = [rs for rs in hosts if rack_of(rs) == rack_of(hosts[0])]
+    far = [rs for rs in hosts if rack_of(rs) != rack_of(hosts[0])]
+    near_ranks = [r for rs in near for r in rs]
+    far_ranks = [r for rs in far for r in rs]
+    calls = {r: [] for r in range(n)}
+    group = {r: None for r in range(n)}
+
+    def gather(mem):
+        for i, r in enumerate(mem):
+            group[r] = mem
+            calls[r].append(("S", "sg%d" % i, i, [mem[(i + d) % len(mem)] for d in range(1, len(mem))]))
+
+    for gi in range(2):
+        mem = [rs[2 * gi + b] for rs in near for b in range(2)]
+        gather(mem)
+        for i, r in enumerate(mem):
+            later = [x for x in near_ranks if x > r and x not in mem]
+            if i % 2:
+                later = [later[j ^ 1] for j in range(len(later))]
+            if later:
+                calls[r].append(("S", "sw", 4 + i, later))
+            cross = [d for d in far_ranks if topo.may_write(cores[r], cores[d]) and pos[d] % 2 == pos[r] % 2]
+            cross.sort(key=lambda d: topo.chip(cores[d]) != topo.chip(cores[r]))
+            calls[r].append(("G", "st%d" % gi, 8 + gi, cross))
+    gather(far[0])
+    for r in far[0]:
+        calls[r].append(("G", "sh", 10, [far[1][pos[r]]]))
+    for r in far[1]:
+        later = [x for x in far[1] if x > r]
+        if later:
+            calls[r].append(("S", "sw", 4 + pos[r], later))
+    return calls, group
+
+
+def _terms(calls, group, r):
+    got = []
+    for s in calls:
+        place = 0
+        for what, sem, slot, dsts in calls[s]:
+            if what == "G":
+                place = 0
+            for d in dsts:
+                place += 1
+                if d == r:
+                    got.append((0 if what == "S" else 1, place, sem, slot, {s} if what == "S" else set(group[s]), s))
+    got.sort(key=lambda t: (t[0], t[1], -t[3]))
+    return got
+
+
+def rank_program(g, core, T, topo):
+    r = T.rank_of(core)
+    if r is None:
+        return
+    cores = list(T.cores)
+    calls, group = _plan(cores, topo)
+    mine, mem, got = calls[r], group[r], _terms(calls, group, r)
+    S, te, ve = T.sem, g.tensor, g.vector
+    slot = lambda i: T.land[:, i * B:(i + 1) * B]
+    engines = lambda m: bin(m).count("1")
+    width = {}
+    for _, _, sem, _, _, s in got:
+        width[sem] = width.get(sem, 0) + engines(topo.mask(cores[s], core))
+    use = [t for t in got if max(t[4]) < r]
+    seen = sorted(b for t in use for b in t[4])
+    assert seen == list(range(r)), (r, seen)
+
+    nkv = 16
+    if mine:
+        g.sync.dma_start(T.kt_sb[:], T.kt[:]).then_inc(S.lkv, 16)
+        nkv = 32
+    g.scalar.dma_start(T.v_sb[:], T.v[:]).then_inc(S.lkv, 16)
+    g.sync.dma_start(T.q_sb[:], T.q[:]).then_inc(S.lqk, 16)
+    g.scalar.dma_start(T.k_sb[:], T.k[:]).then_inc(S.lqk, 16)
+    g.sync.dma_start(T.m_sb[:], T.m[:]).then_inc(S.lm, 16)
+
+    te.wait_ge(S.lkv, nkv)
+    if mine:
+        te.matmul(T.ps_s[:, 0:B], T.kt_sb[:], T.v_sb[:], True, True).then_inc(S.ps, 1)
+    te.wait_ge(S.lqk, 32)
+    te.matmul(T.ps_a[:, 0:B], T.k_sb[:], T.q_sb[:], True, True).then_inc(S.pa, 1)
+    te.wait_ge(S.va, 1)
+    last = te.matmul(T.ps_y[:, 0:B], T.v_sb[:], T.am_bf[:], True, not use)
+    waited = set()
+    for i, t in enumerate(use):
+        if t[2] not in waited:
+            te.wait_ge(S[t[2]], width[t[2]])
+            waited.add(t[2])
+        last = te.matmul(T.ps_y[:, 0:B], slot(t[3]), T.q_sb[:], False, i == len(use) - 1)
+    last.then_inc(S.py, 1)
+
+    if mine:
+        ve.wait_ge(S.ps, 1)
+        ve.tensor_copy(T.s_bf[:], T.ps_s[:, 0:B]).then_inc(S.vs, 1)
+    ve.wait_ge(S.pa, 1)
+    ve.wait_ge(S.lm, 16)
+    ve.tensor_tensor(T.am_bf[:], T.ps_a[:, 0:B], T.m_sb[:], AluOpType.mult).then_inc(S.va, 1)
+    if mem:
+        i = mem.index(r)
+        acc = T.ps_s[:, 0:B]
+        for d in range(1, len(mem)):
+            j = (i - d) % len(mem)
+            ve.wait_ge(S["sg%d" % j], width["sg%d" % j])
+            if d > 1:
+                ve.wait_ge(S.vc, d - 1)
+            if d < len(mem) - 1:
+                out = T.ps_c[:, (d - 1) * B:d * B]
+                ve.tensor_tensor(out, acc, slot(j), AluOpType.add).then_inc(S.vc, 1)
+                acc = out
+            else:
+                ve.tensor_tensor(T.gs_bf[:], acc, slot(j), AluOpType.add).then_inc(S.vg, 1)
+    ve.wait_ge(S.py, 1)
+    ve.tensor_copy(T.y_sb[:], T.ps_y[:, 0:B]).then_inc(S.vy, 1)
+
+    left = 0
+    state = None
+    for what, sem, sl, dsts in mine:
+        if what != state:
+            g.wait_ge(S.vs if what == "S" else S.vg, 1)
+            state = what
+        mask = topo.mask(core, cores[dsts[0]])
+        ids = []
+        for d in dsts:
+            mask &= topo.mask(core, cores[d])
+            rid, pid = topo.addr(cores[d], core)
+            ids.append(DstId(rid=rid, pnc=pid))
+        g.remote_dma_fused([RemoteDMATransfer(dst_ids=ids, dma_engine_mask=mask, remote_sem=S[sem],
+                                              srcs=[T.s_bf[:] if what == "S" else T.gs_bf[:]],
+                                              dsts=[slot(sl) for _ in dsts], alu_op=0)], local_sem=S.sent)
+        left += engines(mask)
+    if left:
+        g.wait_ge(S.sent, left)
+
+    g.sync.wait_ge(S.vy, 1)
+    g.sync.dma_start(T.y[:], T.y_sb[:]).then_inc(S.sty, 16)
+    g.sync.wait_ge(S.sty, 16)

@@ -2,25 +2,30 @@ from concourse.bass import DstId, RemoteDMATransfer
 from concourse.mybir import AluOpType
 
 B = 128
+H = B // 2
 NSLOT = 11
 SCRATCH = {
-    "kt_sb": ("sbuf", [B, B], "bfloat16"),
-    "v_sb": ("sbuf", [B, B], "bfloat16"),
+    "kv_sb": ("sbuf", [B, 2 * B], "bfloat16"),
+    "raw": ("sbuf", [B, 2 * B], "bfloat16"),
     "q_sb": ("sbuf", [B, B], "bfloat16"),
     "k_sb": ("sbuf", [B, B], "bfloat16"),
     "m_sb": ("sbuf", [B, B], "bfloat16"),
     "s_bf": ("sbuf", [B, B], "bfloat16"),
     "am_bf": ("sbuf", [B, B], "bfloat16"),
+    "pt_bf": ("sbuf", [B, B], "bfloat16"),
     "gs_bf": ("sbuf", [B, B], "bfloat16"),
     "y_sb": ("sbuf", [B, B], "bfloat16"),
     "land": ("sbuf", [B, NSLOT * B], "bfloat16"),
     "ps_s": ("psum", [B, 512], "float32"),
     "ps_a": ("psum", [B, 512], "float32"),
-    "ps_y": ("psum", [B, 512], "float32"),
-    "ps_c": ("psum", [B, 512], "float32"),
+    "ps_y0": ("psum", [B, 512], "float32"),
+    "ps_y1": ("psum", [B, 512], "float32"),
+    "ps_g0": ("psum", [B, 512], "float32"),
+    "ps_g1": ("psum", [B, 512], "float32"),
+    "ps_r": ("psum", [B, 512], "float32"),
 }
-SEMAPHORES = ["lkv", "lqk", "lm", "ps", "pa", "py", "vs", "va", "vc", "vg", "vy", "sty", "sent",
-              "sg0", "sg1", "sg2", "sg3", "sw", "st0", "st1", "sh"]
+SEMAPHORES = ["lkv", "lqk", "lm", "ps", "pa", "pr0", "pr1", "pq", "py0", "py1", "vs", "va", "vr", "vt", "vg", "vy", "sty", "sent",
+              "sr", "sg0", "sg1", "sg2", "sg3", "sw", "st0", "st1", "sh"]
 
 
 def _plan(cores, topo):
@@ -42,19 +47,24 @@ def _plan(cores, topo):
     def gather(mem):
         for i, r in enumerate(mem):
             group[r] = mem
-            calls[r].append(("S", "sg%d" % i, i, [mem[(i + d) % len(mem)] for d in range(1, len(mem))]))
+            calls[r].append(("R", "sr", i, [mem[i ^ 1]]))
+            calls[r].append(("S", "sg%d" % i, i, [mem[i ^ 2], mem[i ^ 3]]))
 
     for gi in range(2):
         mem = [rs[2 * gi + b] for rs in near for b in range(2)]
         gather(mem)
+        after = [x for x in near_ranks if x > max(mem)]
+        free = [x for x in mem if not [y for y in near_ranks if y > x and y not in mem and y not in after]]
         for i, r in enumerate(mem):
-            later = [x for x in near_ranks if x > r and x not in mem]
+            later = [x for x in near_ranks if x > r and x not in mem and x not in after]
             if i % 2:
                 later = [later[j ^ 1] for j in range(len(later))]
             if later:
                 calls[r].append(("S", "sw", 4 + i, later))
             cross = [d for d in far_ranks if topo.may_write(cores[r], cores[d]) and pos[d] % 2 == pos[r] % 2]
             cross.sort(key=lambda d: topo.chip(cores[d]) != topo.chip(cores[r]))
+            if r in free:
+                cross = cross + after[free.index(r)::len(free)]
             calls[r].append(("G", "st%d" % gi, 8 + gi, cross))
     gather(far[0])
     for r in far[0]:
@@ -74,9 +84,10 @@ def _terms(calls, group, r):
             if what == "G":
                 place = 0
             for d in dsts:
-                place += 1
+                place += 2 if what == "R" else 1
                 if d == r:
-                    got.append((0 if what == "S" else 1, place, sem, slot, {s} if what == "S" else set(group[s]), s))
+                    got.append((1 if what == "G" else 0, 4 if what == "R" else place, sem, slot,
+                                set(group[s]) if what == "G" else {s}, s, what))
     got.sort(key=lambda t: (t[0], t[1], -t[3]))
     return got
 
@@ -90,37 +101,59 @@ def rank_program(g, core, T, topo):
     mine, mem, got = calls[r], group[r], _terms(calls, group, r)
     S, te, ve = T.sem, g.tensor, g.vector
     slot = lambda i: T.land[:, i * B:(i + 1) * B]
+    kt_sb, v_sb = T.kv_sb[:, 0:B], T.kv_sb[:, B:2 * B]
     engines = lambda m: bin(m).count("1")
     width = {}
-    for _, _, sem, _, _, s in got:
-        width[sem] = width.get(sem, 0) + engines(topo.mask(cores[s], core))
+    for t in got:
+        width[t[2]] = width.get(t[2], 0) + engines(topo.mask(cores[t[5]], core))
     use = [t for t in got if max(t[4]) < r]
     seen = sorted(b for t in use for b in t[4])
     assert seen == list(range(r)), (r, seen)
+    i = mem.index(r) if mem else None
+    need_raw_s = bool(mem) and any(t[6] == "R" for t in use)
+    nsum = max([len(c[3]) for c in mine if c[0] == "G"] + [0])
+    ybank = [T.ps_y0[:, 0:H], T.ps_y1[:, 0:H]]
+    gbank = [T.ps_g0[:, 0:H], T.ps_g1[:, 0:H]]
 
     nkv = 16
     if mine:
-        g.sync.dma_start(T.kt_sb[:], T.kt[:]).then_inc(S.lkv, 16)
+        g.sync.dma_start(kt_sb, T.kt[:]).then_inc(S.lkv, 16)
         nkv = 32
-    g.scalar.dma_start(T.v_sb[:], T.v[:]).then_inc(S.lkv, 16)
+    g.scalar.dma_start(v_sb, T.v[:]).then_inc(S.lkv, 16)
     g.sync.dma_start(T.q_sb[:], T.q[:]).then_inc(S.lqk, 16)
     g.scalar.dma_start(T.k_sb[:], T.k[:]).then_inc(S.lqk, 16)
     g.sync.dma_start(T.m_sb[:], T.m[:]).then_inc(S.lm, 16)
 
+    def y_term(lhsT, rhs, start, stop):
+        for h in range(2):
+            mm = te.matmul(ybank[h], lhsT, rhs[:, h * H:(h + 1) * H], start, stop)
+            if stop:
+                mm.then_inc(S["py%d" % h], 1)
+
     te.wait_ge(S.lkv, nkv)
     if mine:
-        te.matmul(T.ps_s[:, 0:B], T.kt_sb[:], T.v_sb[:], True, True).then_inc(S.ps, 1)
+        te.matmul(T.ps_s[:, 0:B], kt_sb, v_sb, True, True).then_inc(S.ps, 1)
+    if mem:
+        for h in range(2):
+            te.matmul(gbank[h], kt_sb, T.kv_sb[:, B + h * H:B + (h + 1) * H], True, False)
     te.wait_ge(S.lqk, 32)
     te.matmul(T.ps_a[:, 0:B], T.k_sb[:], T.q_sb[:], True, True).then_inc(S.pa, 1)
     te.wait_ge(S.va, 1)
-    last = te.matmul(T.ps_y[:, 0:B], T.v_sb[:], T.am_bf[:], True, not use)
+    y_term(v_sb, T.am_bf, True, not use)
+    if mem:
+        te.wait_ge(S.sr, width["sr"])
+        for h in range(2):
+            te.matmul(gbank[h], T.raw[:, 0:B], T.raw[:, B + h * H:B + (h + 1) * H], False, True).then_inc(S["pr%d" % h], 1)
+        if need_raw_s:
+            te.matmul(T.ps_r[:, 0:B], T.raw[:, 0:B], T.raw[:, B:2 * B], True, True).then_inc(S.pq, 1)
     waited = set()
-    for i, t in enumerate(use):
-        if t[2] not in waited:
+    for n, t in enumerate(use):
+        if t[6] == "R":
+            te.wait_ge(S.vr, 1)
+        elif t[2] not in waited:
             te.wait_ge(S[t[2]], width[t[2]])
             waited.add(t[2])
-        last = te.matmul(T.ps_y[:, 0:B], slot(t[3]), T.q_sb[:], False, i == len(use) - 1)
-    last.then_inc(S.py, 1)
+        y_term(slot(t[3]), T.q_sb, False, n == len(use) - 1)
 
     if mine:
         ve.wait_ge(S.ps, 1)
@@ -129,41 +162,57 @@ def rank_program(g, core, T, topo):
     ve.wait_ge(S.lm, 16)
     ve.tensor_tensor(T.am_bf[:], T.ps_a[:, 0:B], T.m_sb[:], AluOpType.mult).then_inc(S.va, 1)
     if mem:
-        i = mem.index(r)
-        acc = T.ps_s[:, 0:B]
-        for d in range(1, len(mem)):
-            j = (i - d) % len(mem)
-            ve.wait_ge(S["sg%d" % j], width["sg%d" % j])
-            if d > 1:
-                ve.wait_ge(S.vc, d - 1)
-            if d < len(mem) - 1:
-                out = T.ps_c[:, (d - 1) * B:d * B]
-                ve.tensor_tensor(out, acc, slot(j), AluOpType.add).then_inc(S.vc, 1)
-                acc = out
-            else:
-                ve.tensor_tensor(T.gs_bf[:], acc, slot(j), AluOpType.add).then_inc(S.vg, 1)
-    ve.wait_ge(S.py, 1)
-    ve.tensor_copy(T.y_sb[:], T.ps_y[:, 0:B]).then_inc(S.vy, 1)
+        j2, j3 = i ^ 2, i ^ 3
+        ve.wait_ge(S["sg%d" % j2], width["sg%d" % j2])
+        for h in range(2):
+            ve.wait_ge(S["pr%d" % h], 1)
+            ve.tensor_tensor(T.pt_bf[:, h * H:(h + 1) * H], gbank[h], T.land[:, j2 * B + h * H:j2 * B + (h + 1) * H],
+                             AluOpType.add).then_inc(S.vt, 1)
+        if nsum > 1:
+            ve.wait_ge(S["sg%d" % j3], width["sg%d" % j3])
+            ve.wait_ge(S.vt, 2)
+            ve.tensor_tensor(T.gs_bf[:], T.pt_bf[:], slot(j3), AluOpType.add).then_inc(S.vg, 1)
+        if need_raw_s:
+            ve.wait_ge(S.pq, 1)
+            ve.tensor_copy(slot(i ^ 1), T.ps_r[:, 0:B]).then_inc(S.vr, 1)
+    for h in range(2):
+        ve.wait_ge(S["py%d" % h], 1)
+        ve.tensor_copy(T.y_sb[:, h * H:(h + 1) * H], ybank[h]).then_inc(S.vy, 1)
 
-    left = 0
-    state = None
-    for what, sem, sl, dsts in mine:
-        if what != state:
-            g.wait_ge(S.vs if what == "S" else S.vg, 1)
-            state = what
+    left = [0]
+
+    def send(srcs, sem, out, dsts):
         mask = topo.mask(core, cores[dsts[0]])
         ids = []
         for d in dsts:
             mask &= topo.mask(core, cores[d])
             rid, pid = topo.addr(cores[d], core)
             ids.append(DstId(rid=rid, pnc=pid))
-        g.remote_dma_fused([RemoteDMATransfer(dst_ids=ids, dma_engine_mask=mask, remote_sem=S[sem],
-                                              srcs=[T.s_bf[:] if what == "S" else T.gs_bf[:]],
-                                              dsts=[slot(sl) for _ in dsts], alu_op=0)], local_sem=S.sent)
-        left += engines(mask)
-    if left:
-        g.wait_ge(S.sent, left)
+        g.remote_dma_fused([RemoteDMATransfer(dst_ids=ids, dma_engine_mask=mask, remote_sem=S[sem], srcs=srcs,
+                                              dsts=[out for _ in dsts], alu_op=1 if len(srcs) > 1 else 0)], local_sem=S.sent)
+        left[0] += engines(mask)
 
-    g.sync.wait_ge(S.vy, 1)
+    have_s = False
+    for what, sem, sl, dsts in mine:
+        if what == "R":
+            g.wait_ge(S.lkv, nkv)
+            send([T.kv_sb[:]], sem, T.raw[:], dsts)
+        elif what == "S":
+            if not have_s:
+                g.wait_ge(S.vs, 1)
+                have_s = True
+            send([T.s_bf[:]], sem, slot(sl), dsts)
+        else:
+            j3 = i ^ 3
+            g.wait_ge(S["sg%d" % j3], width["sg%d" % j3])
+            g.wait_ge(S.vt, 2)
+            send([T.pt_bf[:], slot(j3)], sem, slot(sl), dsts[:1])
+            if dsts[1:]:
+                g.wait_ge(S.vg, 1)
+                send([T.gs_bf[:]], sem, slot(sl), dsts[1:])
+    if left[0]:
+        g.wait_ge(S.sent, left[0])
+
+    g.sync.wait_ge(S.vy, 2)
     g.sync.dma_start(T.y[:], T.y_sb[:]).then_inc(S.sty, 16)
     g.sync.wait_ge(S.sty, 16)

from concourse.bass import DstId, RemoteDMATransfer
from concourse.mybir import AluOpType

B = 128
H = B // 2
NSLOT = 11
SCRATCH = {
    "kv_sb": ("sbuf", [B, 2 * B], "bfloat16"),
    "raw": ("sbuf", [B, 2 * B], "bfloat16"),
    "q_sb": ("sbuf", [B, B], "bfloat16"),
    "k_sb": ("sbuf", [B, B], "bfloat16"),
    "m_sb": ("sbuf", [B, B], "bfloat16"),
    "s_bf": ("sbuf", [B, B], "bfloat16"),
    "am_bf": ("sbuf", [B, B], "bfloat16"),
    "pt_bf": ("sbuf", [B, B], "bfloat16"),
    "gs_bf": ("sbuf", [B, B], "bfloat16"),
    "y_sb": ("sbuf", [B, B], "bfloat16"),
    "land": ("sbuf", [B, NSLOT * B], "bfloat16"),
    "ps_s": ("psum", [B, 512], "float32"),
    "ps_a": ("psum", [B, 512], "float32"),
    "ps_y0": ("psum", [B, 512], "float32"),
    "ps_y1": ("psum", [B, 512], "float32"),
    "ps_g0": ("psum", [B, 512], "float32"),
    "ps_g1": ("psum", [B, 512], "float32"),
    "ps_r": ("psum", [B, 512], "float32"),
}
SEMAPHORES = ["lkv", "lqk", "lm", "ps", "pa", "pr0", "pr1", "pq", "py0", "py1", "vs", "va", "vr", "vt", "vg", "vy", "sty", "sent",
              "sr", "sg0", "sg1", "sg2", "sg3", "sw", "st0", "st1", "sh"]


def _plan(cores, topo):
    n = len(cores)
    hosts = []
    for r, c in enumerate(cores):
        if not hosts or topo.host(cores[hosts[-1][0]]) != topo.host(c):
            hosts.append([])
        hosts[-1].append(r)
    pos = {r: i for rs in hosts for i, r in enumerate(rs)}
    rack_of = lambda rs: topo.rack(topo.host(cores[rs[0]]))
    near = [rs for rs in hosts if rack_of(rs) == rack_of(hosts[0])]
    far = [rs for rs in hosts if rack_of(rs) != rack_of(hosts[0])]
    near_ranks = [r for rs in near for r in rs]
    far_ranks = [r for rs in far for r in rs]
    calls = {r: [] for r in range(n)}
    group = {r: None for r in range(n)}

    def gather(mem):
        for i, r in enumerate(mem):
            group[r] = mem
            calls[r].append(("R", "sr", i, [mem[i ^ 1]]))
            calls[r].append(("S", "sg%d" % i, i, [mem[i ^ 2], mem[i ^ 3]]))

    for gi in range(2):
        mem = [rs[2 * gi + b] for rs in near for b in range(2)]
        gather(mem)
        after = [x for x in near_ranks if x > max(mem)]
        free = [x for x in mem if not [y for y in near_ranks if y > x and y not in mem and y not in after]]
        for i, r in enumerate(mem):
            later = [x for x in near_ranks if x > r and x not in mem and x not in after]
            if i % 2:
                later = [later[j ^ 1] for j in range(len(later))]
            if later:
                calls[r].append(("S", "sw", 4 + i, later))
            cross = [d for d in far_ranks if topo.may_write(cores[r], cores[d]) and pos[d] % 2 == pos[r] % 2]
            cross.sort(key=lambda d: topo.chip(cores[d]) != topo.chip(cores[r]))
            if r in free:
                cross = cross + after[free.index(r)::len(free)]
            calls[r].append(("G", "st%d" % gi, 8 + gi, cross))
    gather(far[0])
    for r in far[0]:
        calls[r].append(("G", "sh", 10, [far[1][pos[r]]]))
    for r in far[1]:
        later = [x for x in far[1] if x > r]
        if later:
            calls[r].append(("S", "sw", 4 + pos[r], later))
    return calls, group


def _terms(calls, group, r):
    got = []
    for s in calls:
        place = 0
        for what, sem, slot, dsts in calls[s]:
            if what == "G":
                place = 0
            for d in dsts:
                place += 2 if what == "R" else 1
                if d == r:
                    got.append((1 if what == "G" else 0, 4 if what == "R" else place, sem, slot,
                                set(group[s]) if what == "G" else {s}, s, what))
    got.sort(key=lambda t: (t[0], t[1], -t[3]))
    return got


def rank_program(g, core, T, topo):
    r = T.rank_of(core)
    if r is None:
        return
    cores = list(T.cores)
    calls, group = _plan(cores, topo)
    mine, mem, got = calls[r], group[r], _terms(calls, group, r)
    S, te, ve = T.sem, g.tensor, g.vector
    slot = lambda i: T.land[:, i * B:(i + 1) * B]
    kt_sb, v_sb = T.kv_sb[:, 0:B], T.kv_sb[:, B:2 * B]
    engines = lambda m: bin(m).count("1")
    width = {}
    for t in got:
        width[t[2]] = width.get(t[2], 0) + engines(topo.mask(cores[t[5]], core))
    use = [t for t in got if max(t[4]) < r]
    seen = sorted(b for t in use for b in t[4])
    assert seen == list(range(r)), (r, seen)
    i = mem.index(r) if mem else None
    need_raw_s = bool(mem) and any(t[6] == "R" for t in use)
    nsum = max([len(c[3]) for c in mine if c[0] == "G"] + [0])
    ybank = [T.ps_y0[:, 0:H], T.ps_y1[:, 0:H]]
    gbank = [T.ps_g0[:, 0:H], T.ps_g1[:, 0:H]]

    nkv = 16
    if mine:
        g.sync.dma_start(kt_sb, T.kt[:]).then_inc(S.lkv, 16)
        nkv = 32
    g.scalar.dma_start(v_sb, T.v[:]).then_inc(S.lkv, 16)
    g.sync.dma_start(T.q_sb[:], T.q[:]).then_inc(S.lqk, 16)
    g.scalar.dma_start(T.k_sb[:], T.k[:]).then_inc(S.lqk, 16)
    g.sync.dma_start(T.m_sb[:], T.m[:]).then_inc(S.lm, 16)

    def y_term(lhsT, rhs, start, stop):
        for h in range(2):
            mm = te.matmul(ybank[h], lhsT, rhs[:, h * H:(h + 1) * H], start, stop)
            if stop:
                mm.then_inc(S["py%d" % h], 1)

    te.wait_ge(S.lkv, nkv)
    if mine:
        te.matmul(T.ps_s[:, 0:B], kt_sb, v_sb, True, True).then_inc(S.ps, 1)
    if mem:
        for h in range(2):
            te.matmul(gbank[h], kt_sb, T.kv_sb[:, B + h * H:B + (h + 1) * H], True, False)
    te.wait_ge(S.lqk, 32)
    te.matmul(T.ps_a[:, 0:B], T.k_sb[:], T.q_sb[:], True, True).then_inc(S.pa, 1)
    te.wait_ge(S.va, 1)
    y_term(v_sb, T.am_bf, True, not use)
    if mem:
        te.wait_ge(S.sr, width["sr"])
        for h in range(2):
            te.matmul(gbank[h], T.raw[:, 0:B], T.raw[:, B + h * H:B + (h + 1) * H], False, True).then_inc(S["pr%d" % h], 1)
        if need_raw_s:
            te.matmul(T.ps_r[:, 0:B], T.raw[:, 0:B], T.raw[:, B:2 * B], True, True).then_inc(S.pq, 1)
    waited = set()
    for n, t in enumerate(use):
        if t[6] == "R":
            te.wait_ge(S.vr, 1)
        elif t[2] not in waited:
            te.wait_ge(S[t[2]], width[t[2]])
            waited.add(t[2])
        y_term(slot(t[3]), T.q_sb, False, n == len(use) - 1)

    if mine:
        ve.wait_ge(S.ps, 1)
        ve.tensor_copy(T.s_bf[:], T.ps_s[:, 0:B]).then_inc(S.vs, 1)
    ve.wait_ge(S.pa, 1)
    ve.wait_ge(S.lm, 16)
    ve.tensor_tensor(T.am_bf[:], T.ps_a[:, 0:B], T.m_sb[:], AluOpType.mult).then_inc(S.va, 1)
    if mem:
        j2, j3 = i ^ 2, i ^ 3
        ve.wait_ge(S["sg%d" % j2], width["sg%d" % j2])
        for h in range(2):
            ve.wait_ge(S["pr%d" % h], 1)
            ve.tensor_tensor(T.pt_bf[:, h * H:(h + 1) * H], gbank[h], T.land[:, j2 * B + h * H:j2 * B + (h + 1) * H],
                             AluOpType.add).then_inc(S.vt, 1)
        if nsum > 1:
            ve.wait_ge(S["sg%d" % j3], width["sg%d" % j3])
            ve.wait_ge(S.vt, 2)
            ve.tensor_tensor(T.gs_bf[:], T.pt_bf[:], slot(j3), AluOpType.add).then_inc(S.vg, 1)
        if need_raw_s:
            ve.wait_ge(S.pq, 1)
            ve.tensor_copy(slot(i ^ 1), T.ps_r[:, 0:B]).then_inc(S.vr, 1)
    for h in range(2):
        ve.wait_ge(S["py%d" % h], 1)
        ve.tensor_copy(T.y_sb[:, h * H:(h + 1) * H], ybank[h]).then_inc(S.vy, 1)

    left = [0]

    def send(srcs, sem, out, dsts):
        mask = topo.mask(core, cores[dsts[0]])
        ids = []
        for d in dsts:
            mask &= topo.mask(core, cores[d])
            rid, pid = topo.addr(cores[d], core)
            ids.append(DstId(rid=rid, pnc=pid))
        g.remote_dma_fused([RemoteDMATransfer(dst_ids=ids, dma_engine_mask=mask, remote_sem=S[sem], srcs=srcs,
                                              dsts=[out for _ in dsts], alu_op=1 if len(srcs) > 1 else 0)], local_sem=S.sent)
        left[0] += engines(mask)

    have_s = False
    for what, sem, sl, dsts in mine:
        if what == "R":
            g.wait_ge(S.lkv, nkv)
            send([T.kv_sb[:]], sem, T.raw[:], dsts)
        elif what == "S":
            if not have_s:
                g.wait_ge(S.vs, 1)
                have_s = True
            send([T.s_bf[:]], sem, slot(sl), dsts)
        else:
            j3 = i ^ 3
            g.wait_ge(S["sg%d" % j3], width["sg%d" % j3])
            g.wait_ge(S.vt, 2)
            send([T.pt_bf[:], slot(j3)], sem, slot(sl), dsts[:1])
            if dsts[1:]:
                g.wait_ge(S.vg, 1)
                send([T.gs_bf[:]], sem, slot(sl), dsts[1:])
    if left[0]:
        g.wait_ge(S.sent, left[0])

    g.sync.wait_ge(S.vy, 2)
    g.sync.dma_start(T.y[:], T.y_sb[:]).then_inc(S.sty, 16)
    g.sync.wait_ge(S.sty, 16)
